import numpy as np, ml_dtypes
CORES = [35,38,43,46]
N = 4
BF = ml_dtypes.bfloat16
def gentries(a):
    return np.ascontiguousarray(a.reshape(8, 16, -1).transpose(0, 2, 1)).reshape(8, -1)
def gtable(e):
    e = np.asarray(e); return np.ascontiguousarray(e.reshape(8, -1, 16).transpose(0, 2, 1)).reshape(128, -1).astype(np.int32)
D, UG, B, A, NB, KG = 3, 16, 6, 2, 32, 16
U, V, E, S, K = 8 * UG, 2 ** B, 2 ** (A * B), 16 * NB, 8 * KG // N
def stored(c):
    return np.ascontiguousarray(c.reshape(N, 8, UG, NB, 16).transpose(0, 1, 4, 3, 2)).reshape(N, 128, -1).astype(np.int32)
def unstored(x):
    return np.ascontiguousarray(x.reshape(N, 8, 16, NB, UG).transpose(0, 1, 4, 3, 2)).reshape(N, U, S).astype(np.int64)
def pack(t, c, gv, wr):
    return {"tb": t.reshape(N, 8, -1).astype(np.float32).astype(BF), "x": stored(c), "give": np.stack([gtable(v.reshape(8, -1)) for v in gv]), "wires": np.stack([gtable(v.reshape(8, -1)) for v in wr])}
def draw(rng):
    return rng.integers(0, V, (N, 8, D, UG, E)), rng.integers(0, V, (N, U, S)), rng.integers(0, U, (N, 8, D, KG)), rng.integers(0, N * K, (N, 8, D, A, UG))
def setup_inputs(rng):
    return pack(*draw(rng))
def setup_inputs_ends(rng):
    t, c, gv, wr = draw(rng)
    t = rng.integers(0, 2, t.shape) * (V - 1); t[..., 0] = 0; t[..., E - 1] = V - 1; c = rng.integers(0, 2, c.shape) * (V - 1); c[:, :, 0] = 0; c[:, :, S - 1] = V - 1
    gv = rng.choice(np.array([0, UG - 1, UG, 7 * UG, U - 1]), gv.shape); wr = rng.choice(np.array([0, K - 1, K, N * K - K, N * K - 1]), wr.shape)
    return pack(t, c, gv, wr)
def setup_inputs_one(rng):
    t, c, gv, wr = draw(rng)
    gv[:] = gv[..., :1].copy(); wr[:] = wr[:, :, :, :1].copy(); q = rng.integers(0, N); wr[q] = wr[q][..., :1].copy()
    return pack(t, c, gv, wr)
def setup_inputs_next(rng):
    t, c, gv, wr = draw(rng)
    i = rng.integers(0, 2, (N, 8, D, UG, 1)) * (A - 1); t = (np.arange(E) >> (B * (A - 1 - i))) & (V - 1)
    wr = wr % K + K * ((np.arange(N) + 1) % N).reshape(N, 1, 1, 1, 1)
    return pack(t, c, gv, wr)
def setup_inputs_spread(rng):
    t, c, gv, wr = draw(rng)
    t = t >> rng.integers(0, B + 1, (N, 8, D, UG, 1)); c = c >> rng.integers(0, B + 1, (N, U, 1))
    gv = (rng.random(gv.shape) ** 3 * U).astype(np.int64); wr = (rng.random(wr.shape) ** 3 * (N * K)).astype(np.int64)
    return pack(t, c, gv, wr)
def check_inputs(d):
    bad = []
    for name, top in (("x", V), ("give", U), ("wires", N * K)):
        if not ((d[name] >= 0) & (d[name] < top)).all(): bad.append(name)
    t = d["tb"].astype(np.float32)
    if not ((t >= 0) & (t < V) & (np.floor(t) == t)).all(): bad.append("tb")
    return bad
def reference(tb, x, give, wires):
    t = tb.astype(np.float32).astype(np.int64).reshape(N, 8, D, UG, E)
    gv = np.stack([gentries(v) for v in give]).reshape(N, 8 * D * KG).reshape(N, 8, D, KG)
    wr = np.stack([gentries(v) for v in wires]).reshape(N, 8, D, A, UG)
    c = unstored(x)
    for l in range(D):
        lines = np.zeros((N, N * K, S), np.int64); new = np.zeros((N, U, S), np.int64)
        for q in range(N):
            lines[:, q * K:(q + 1) * K] = c[q][gv[q, :, l].reshape(-1)].reshape(N, K, S)
        for r in range(N):
            a = np.zeros((8, UG, S), np.int64)
            for i in range(A):
                a = a * V + lines[r][wr[r, :, l, i]]
            new[r] = np.take_along_axis(t[r, :, l], a, axis=2).reshape(U, S)
        c = new
    return {"y": np.asarray(stored(c), np.float32)}

@@ -1,0 +1,360 @@
+from concourse.bass import DstId, RemoteDMATransfer
+from concourse.mybir import AluOpType, ActivationFunctionType
+
+OP = AluOpType
+COPY = ActivationFunctionType.Copy
+NBLK = 4
+NT = 3 * NBLK
+A4 = [[0], [1], [2], [3]]
+SENDS = {0: [[0, 1], [2, 3]], 1: A4, 2: A4}
+CYC, PEC, GAT, FIX, WAKE, REM, DMA = 1.0e-3, 0.5e-3, 1.56e-3, 0.05, 0.06, 4.2, 2.0
+TP, TQ = 2, 2
+GX = 0
+UNITS = [[("v", 0, 40), ("s", 40, 24)], [("v", 64, 20), ("s", 84, 44)]]
+LTQ, ZQ, LSQ = "v", "v", "s"
+
+
+def steps(then, t):
+    then("v", (t, "gv0"), (t - 1, "z"), (t + 1, "lt"), (t, "gv1"), (t + 1, "off"))
+    then("s", (t, "gs0"), (t - 1, "pms"), (t + 1, "ls"), (t, "gs1"))
+    then("p", (t - 1, "m1"), (t - 1, "otr"), (t + 1, "tr"), (t + 1, "a"), (t, "m0"))
+
+
+SCRATCH = {
+    "xi": ("sbuf", [128, 512], "int32"),
+    "gi": ("sbuf", [128, 3], "int32"),
+    "wi": ("sbuf", [128, 6], "int32"),
+    "tab": ("sbuf", [128, 3, 4096], "bfloat16"),
+    "jc": ("sbuf", [128, 128], "bfloat16"),
+    "jl": ("sbuf", [128, 128], "bfloat16"),
+    "pint": ("sbuf", [128, 4], "int32"),
+    "pc": ("sbuf", [128, 4], "float32"),
+    "pf": ("sbuf", [128, 1], "float32"),
+    "pbits": ("sbuf", [128, 4], "float32"),
+    "m16": ("sbuf", [128, 16], "float32"),
+    "vc": ("sbuf", [128, 4], "float32"),
+    "ident": ("sbuf", [128, 128], "bfloat16"),
+    "id4": ("sbuf", [128, 4, 2, 16], "bfloat16"),
+    "pall": ("sbuf", [128, 2, 2, 4, 2, 16], "bfloat16"),
+    "ones": ("sbuf", [128, 128], "bfloat16"),
+    "msk": ("sbuf", [128, 16, 128], "bfloat16"),
+    "gf": ("sbuf", [128, 4], "float32"),
+    "wf": ("sbuf", [128, 6], "float32"),
+    "dg": ("sbuf", [128, 3, 128], "bfloat16"),
+    "nbs": ("sbuf", [128, 2, 128], "bfloat16"),
+    "selp": ("sbuf", [128, 4, 128], "bfloat16"),
+    "sel": ("sbuf", [128, 2, 16, 128], "bfloat16"),
+    "oh": ("sbuf", [128, 6, 128], "bfloat16"),
+    "wm": ("sbuf", [128, 3, 128], "bfloat16"),
+    "xb": ("sbuf", [128, 512], "bfloat16"),
+    "xt": ("sbuf", [128, NBLK, 4, 2, 16], "bfloat16"),
+    "ls": ("sbuf", [128, NT, 128], "bfloat16"),
+    "lt": ("sbuf", [128, NT, 128], "bfloat16"),
+    "off": ("sbuf", [128, NT, 128], "uint16"),
+    "gt": ("sbuf", [128, NT, 2048], "bfloat16"),
+    "pms": ("sbuf", [128, NT + NBLK, 4, 2, 16], "bfloat16"),
+    "yo": ("sbuf", [128, 512], "float32"),
+    "q0": ("psum", [128, 8, 128], "bfloat16"),
+    "q1": ("psum", [128, 16, 2, 16], "float32"),
+    "q2": ("psum", [128, 16, 2, 16], "float32"),
+    "pm0": ("psum", [128, 512], "float32"),
+    "pm1": ("psum", [128, 512], "float32"),
+    "pa": ("psum", [128, 512], "float32"),
+    "pt": ("psum", [128, 8, 128], "bfloat16"),
+    "pr": ("psum", [128, 8, 128], "bfloat16"),
+}
+SEMAPHORES = ["v", "p", "s", "k", "x0", "x1", "x2", "x3", "gl", "wl", "t00", "t01", "t10", "t11", "t20", "t21", "yd", "loc"]
+for _e in SENDS:
+    for _c in range(len(SENDS[_e])):
+        SCRATCH["z%d_%d" % (_e, _c)] = ("sbuf", [128, 7, len(SENDS[_e][_c]), 32], "bfloat16")
+        SEMAPHORES.append("a%d_%d" % (_e, _c))
+
+
+def layout(nodes):
+    users = [[] for _ in nodes]
+    for n in nodes:
+        for d in n["deps"]:
+            users[d["i"]].append(n)
+    for n in reversed(nodes):
+        n["cp"] = min(n["dur"].values()) + n["lat"] + max([WAKE + u["cp"] for u in users[n["i"]]] + [0.0])
+    free = {"v": 0.0, "p": 0.0, "s": 0.0, "k": 0.0, "y": 0.0}
+    left = list(nodes)
+    order = []
+    while left:
+        best = None
+        for q in sorted(free):
+            cand = []
+            for n in left:
+                if q in n["dur"] and (n.get("prev") is None or "end" in n["prev"]) and all("end" in d for d in n["deps"]):
+                    cand.append((max([d["end"] + WAKE for d in n["deps"]] + [0.0]), n))
+            if not cand:
+                continue
+            t0 = max(free[q], min(c[0] for c in cand))
+            t, n = min([(-c[1]["cp"] - c[1].get("pri", 0.0), c[1]["i"], max(t0, c[0]), c[1]) for c in cand if c[0] <= t0])[2:]
+            key = (t, t + n["dur"][q], n["i"])
+            if best is None or key < best[0]:
+                best = (key, q, n)
+        (t, e, _), q, n = best
+        n["q"], n["start"], n["end"] = q, t, e + n["lat"]
+        free[q] = e
+        left.remove(n)
+        order.append(n)
+    return order
+
+
+def rank_program(g, core, T, topo):
+    r = T.rank_of(core)
+    if r is None:
+        return
+    cores = T.cores
+    queues = {"v": g.vector, "p": g.tensor, "s": g.scalar, "k": g, "y": g.sync}
+    nodes = []
+
+    def node(dur, deps, emit, sem=None, n=1, lat=0.0):
+        flat = []
+        for d in deps:
+            if isinstance(d, list):
+                flat += [x for x in d if x is not None]
+            elif d is not None:
+                flat.append(d)
+        x = {"i": len(nodes), "dur": dur, "deps": flat, "emit": emit, "sem": sem, "n": n, "lat": lat}
+        nodes.append(x)
+        return x
+
+    def V(deps, name, *a, cy=64):
+        f = {"copy": g.vector.tensor_copy, "ts": g.vector.tensor_scalar, "tr": g.vector.transpose,
+             "set": g.vector.memset}[name]
+        return node({"v": FIX + max(cy, 64) * CYC}, deps, lambda q: f(*a))
+
+    def VS(deps, out, in_, vcy, scy, on="vs"):
+        def emit(q):
+            if q == "v":
+                return g.vector.tensor_copy(out, in_)
+            return g.scalar.activation(out, in_, COPY)
+        dur = {"v": FIX + vcy * CYC, "s": FIX + 0.015 + scy * CYC}
+        return node({q: dur[q] for q in on}, deps, emit)
+
+    def scaled(deps, out, in_, col):
+        def emit(q):
+            if q == "v":
+                return g.vector.tensor_scalar(out, in_, col, None, OP.mult)
+            return g.scalar.activation(out, in_, COPY, scale=col)
+        return node({"v": FIX + 64 * CYC, "s": FIX + 0.015 + 128 * CYC}, deps, emit)
+
+    def MM(deps, calls):
+        def emit(q):
+            for out, lhs, rhs, st, sp, cy in calls:
+                x = g.tensor.matmul(out, lhs, rhs, st, sp)
+            return x
+        return node({"p": 0.02 + sum([c[5] for c in calls]) * PEC}, deps, emit)
+
+    def TR(deps, out, in_):
+        return node({"p": 0.02 + 128 * PEC}, deps, lambda q: g.tensor.transpose(out, in_, T.ident[:]))
+
+    def dma(q, deps, out, in_, s, more=0.0, pri=0.0):
+        x = node({q: 0.05}, deps, lambda qq: queues[qq].dma_start(out, in_), s, 16, DMA + more)
+        x["pri"] = pri
+        return x
+
+    def iota(out, n, pattern, base, cm):
+        return node({"k": 0.13 + 2 * n * CYC}, [], lambda q: g.iota(out, pattern, base, cm, allow_small_or_imprecise_dtypes=True))
+
+    d_give = [dma("s", [], T.gi[32 * c:32 * c + 32, :], T.give[32 * (r ^ c):32 * (r ^ c) + 32, :], "gl") for c in range(4)]
+    d_x = [dma("y", [], T.xi[:, 128 * h:128 * h + 128], T.x[:, 128 * h:128 * h + 128], "x%d" % h, 0.3 * h) for h in range(4)]
+    d_wire = dma("y", [], T.wi[:], T.wires[:], "wl", 1.2)
+    tabs = [[], [], []]
+
+    def load_table(l, h, n, more, deps=()):
+        tabs[l].append(dma("y", list(deps), T.tab[16 * h:16 * h + 16 * n, l, :], T.tb[h:h + n, l * 65536:(l + 1) * 65536],
+                           "t%d%d" % (l, h // n % 2), more, -1000.0))
+
+    load_table(0, 0, 4, 2.5)
+    load_table(0, 4, 4, 4.5)
+
+    s0 = 32 if r % 2 == 0 else -32
+    s1 = 64 if r < 2 else -64
+    k_pint = node({"k": 0.13}, [], lambda q: g.iota(T.pint[:, 0:1], [[0, 1]], 0, 1))
+    k_pc = iota(T.pc[:, 0:3], 3, [[16, 3]], -15, 1)
+    k_pf = iota(T.pf[:], 1, [[0, 1]], 0, 1)
+    k_jc = iota(T.jc[:], 128, [[1, 128]], 0, 0)
+    k_jl = iota(T.jl[:], 128, [[-s1, 2], [-s0, 2], [1, 32]], 32 * (r ^ 3), 0)
+    c_ones = V([], "set", T.ones[:], 1.0)
+    c_pz = V([], "set", T.pall[:], 0.0, cy=256)
+    c_hi = V([k_pint], "ts", T.pint[:, 1:2], T.pint[:, 0:1], 4, 1, OP.arith_shift_right, OP.bitwise_and)
+    c_lo = V([k_pint], "ts", T.pint[:, 2:3], T.pint[:, 0:1], 15, None, OP.bitwise_and)
+    c_bits = V([c_hi, c_lo], "copy", T.pbits[:, 0:2], T.pint[:, 1:3])
+    bit, low = T.pbits[:, 0:1], T.pbits[:, 1:2]
+    c_vc = [V([c_bits, k_pc], "ts", T.vc[:, 0:1], bit, 0.0, T.pc[:, 1:2], OP.is_equal, OP.mult),
+            V([c_bits, k_pc], "ts", T.vc[:, 1:2], bit, 0.0, T.pc[:, 2:3], OP.is_equal, OP.mult),
+            V([c_bits, k_pc], "ts", T.vc[:, 2:3], bit, T.pc[:, 0:1], None, OP.mult),
+            V([c_bits, k_pc], "ts", T.vc[:, 3:4], bit, T.pc[:, 1:2], None, OP.mult)]
+    c_id = V([k_jc, k_pf], "ts", T.ident[:], T.jc[:], T.pf[:], None, OP.is_equal)
+    c_id4 = V([k_jc, k_pf], "ts", T.id4[:], T.jc[:], T.pf[:], None, OP.is_equal)
+    c_m16 = V([k_jc, c_bits], "ts", T.m16[:], T.jc[:, 0:16], low, None, OP.is_equal)
+    c_pall = []
+    for x2 in range(2):
+        for g2 in range(2):
+            c_pall.append(V([c_id4, c_pz], "copy", T.pall[:, x2, g2, :, x2, :], T.id4[:, :, g2, :]))
+
+    dst = {d: cores[r ^ d] for d in (1, 2, 3)}
+    far = [d for d in dst if topo.chip(dst[d]) != topo.chip(core)]
+    near = [d for d in dst if d not in far]
+    use = {}
+    farset = set()
+    for j, d in enumerate(far):
+        en = topo.engines(core, dst[d])
+        farset |= set(en)
+        w = len(en) // len(far)
+        use[d] = en[j * w:j * w + w]
+    for j, d in enumerate(near):
+        en = [x for x in topo.engines(core, dst[d]) if x not in farset]
+        w = len(en) // len(near)
+        use[d] = en[j * w:j * w + w]
+    total_eng = sum(len(use[d]) for d in dst)
+
+    def send(deps, name, src, dest):
+        def emit(q):
+            tr = []
+            for d in (1, 2, 3):
+                rid, pid, _ = topo.addr(dst[d])
+                tr.append(RemoteDMATransfer(dst_ids=[DstId(rid=rid, pnc=pid)], dma_engine_mask=sum(1 << x for x in use[d]),
+                                            remote_sem=T.sem[name], src=src(d), dst=dest(d)))
+            g.remote_dma_fused(tr, local_sem=T.sem.loc)
+            return None
+        return node({"k": 0.6}, deps, emit, name, total_eng, REM - 0.6)
+
+    c_gf = V([d_give], "ts", T.gf[:, 0:3], T.gi[:], 1.0, None, OP.add)
+    c_d = [scaled([c_gf, c_ones], T.dg[:, l, :], T.ones[:], T.gf[:, l:l + 1]) for l in range(3)]
+    m_nb0 = TR([c_d[0], c_id], T.pr[:, 0, :], T.dg[:, 0, :])
+    xt = []
+    for k in range(NBLK):
+        a = V([d_x[k]], "copy", T.xb[:, 128 * k:128 * k + 128], T.xi[:, 128 * k:128 * k + 128], cy=128)
+        xt.append(V([a], "tr", T.xt[:, k], T.xb[:, 128 * k:128 * k + 128]))
+    c_selp = [V([m_nb0, c_vc[v]], "ts", T.selp[:, v, :], T.pr[:, 0, :], T.vc[:, v:v + 1], None, OP.is_equal) for v in range(4)]
+    PV = [(0, 0), (0, 1), (1, 0), (1, 1)]
+    arr, zt = {}, {}
+    free = {"pt": None, "pr": c_selp, "q1": None, "q2": None}
+
+    def zslot(e, k):
+        for ci, blks in enumerate(SENDS[e]):
+            if k in blks:
+                return ci, blks.index(k), blks
+
+    def pack(e, k, dep, bank, on):
+        ci, i, blks = zslot(e, k)
+        z = T["z%d_%d" % (e, ci)]
+        a = TR([dep, c_id] + [free[bank]], T[bank][:, 0, :], T.pms[:, 4 * e + k])
+        free[bank] = zt[(e, k)] = VS([a], z[:, 3:7, i, :], T[bank][:, 0, :], 64, 128, on)
+        if k == blks[-1]:
+            c = send([zt[(e, b)] for b in blks], "a%d_%d" % (e, ci), lambda d: z[:, 3 + d, :, :], lambda d: z[:, 3 - d, :, :])
+            for b in blks:
+                arr[(e, b)] = c
+        return a, zt[(e, k)]
+
+    for k in range(NBLK):
+        q = "q1" if k % 2 == 0 else "q2"
+        a = MM([xt[k], c_selp, free[q]], [(T[q][:, 0:4, bp, :], T.selp[:, 2 * bp + g2, :], T.xt[:, k, :, g2, :], g2 == 0, g2 == 1, 64)
+                                          for bp, g2 in PV])
+        free[q] = VS([a], T.pms[:, k], T[q][:, 0:4], 128, 128)
+        pack(0, k, free[q], "pt" if k % 2 == 0 else "pr", "vs")
+
+    m_nb = [TR([c_d[l], c_id], T.q0[:, l, :], T.dg[:, l, :]) for l in (1, 2)]
+    c_wf = V([d_wire], "copy", T.wf[:], T.wi[:])
+    c_w = []
+    for l in range(3):
+        bank = [T.pa, T.pm0, T.pm1][l]
+        o0 = V([c_wf, k_jl], "ts", T.oh[:, 2 * l, :], T.jl[:], T.wf[:, 2 * l:2 * l + 1], 64.0, OP.is_equal, OP.mult)
+        o1 = V([c_wf, k_jl], "ts", T.oh[:, 2 * l + 1, :], T.jl[:], T.wf[:, 2 * l + 1:2 * l + 2], None, OP.is_equal)
+        a = MM([o0, o1, c_id], [(bank[:, 0:128], T.oh[:, 2 * l, :], T.ident[:], True, False, 128),
+                                (bank[:, 0:128], T.oh[:, 2 * l + 1, :], T.ident[:], False, True, 128)])
+        c_w.append(VS([a], T.wm[:, l, :], bank[:, 0:128], 128, 128))
+    c_one = [V([m_nb, k_pc], "ts", T.nbs[:, l, :], T.q0[:, l + 1, :], T.pc[:, 1:2], None, OP.is_equal) for l in range(2)]
+    c_sel = [[scaled([c_one[l], c_m16], T.sel[:, l, u, :], T.nbs[:, l, :], T.m16[:, u:u + 1]) for u in range(16)] for l in range(2)]
+    c_msk = [scaled([c_m16, c_id], T.msk[:, u, :], T.ident[:], T.m16[:, u:u + 1]) for u in range(16)]
+
+    free.update({"pa": c_w[0], "pm0": c_w[1], "pm1": c_w[2]})
+    B = []
+    for t in range(NT):
+        l, k = divmod(t, NBLK)
+        pm = "pm%d" % (t % 2)
+        o = {}
+        B.append(o)
+        ci, i, blks = zslot(l, k)
+        z = T["z%d_%d" % (l, ci)]
+        if len(blks) > 1:
+            c = o["ls"] = VS([arr[(l, k)], zt[(l, k)]], T.ls[:, t, :], z[:, 0:4, i, :], 64, 128, LSQ)
+            o["tr"] = TR([c, free["pr"], c_id], T.pr[:, 0, :], T.ls[:, t, :])
+        else:
+            o["tr"] = TR([arr[(l, k)], zt[(l, k)], free["pr"], c_id], T.pr[:, 0, :], z[:, 0:4, 0, :])
+        o["lt"] = free["pr"] = VS([o["tr"]], T.lt[:, t, :], T.pr[:, 0, :], 64, 128, LTQ)
+        o["a"] = MM([o["lt"], c_w[l], free["pa"]], [(T.pa[:, 0:128], T.wm[:, l, :], T.lt[:, t, :], True, True, 128)])
+        o["off"] = free["pa"] = V([o["a"]], "copy", T.off[:, t, :], T.pa[:, 0:128], cy=128)
+        if t == 0:
+            for l2 in (1, 2):
+                for h in range(0, 8, TP):
+                    load_table(l2, h, TP, 0.6, [arr[(0, GX)] if l2 == 1 and h < TP * TQ else (tabs[1] + tabs[2])[-TQ]])
+        lhs = [T.msk[:, u, :] if l == 2 else T.sel[:, l, u, :] for u in range(16)]
+        for h in range(2):
+            gs = []
+            for q, b, n in UNITS[h]:
+                gs.append(VS([o["off"], tabs[l]], T.gt[:, t, 16 * b:16 * b + 16 * n], T.tab[:, l, :].indirect(T.off[:, t, b:b + n]),
+                             16 * n * GAT / CYC, 16 * n * GAT / CYC, q))
+                o.setdefault("g%s%d" % (q, h), []).append(gs[-1])
+            o["m%d" % h] = MM([gs, free[pm], c_msk if l == 2 else c_sel[l]],
+                              [(T[pm][:, 64 * h:64 * h + 64], lhs[u], T.gt[:, t, 1024 * h + u:1024 * h + 1024:16], u == 0, u == 15, 64)
+                               for u in range(16)])
+        o["pms"] = free[pm] = VS([o["m0"], o["m1"]], T.pms[:, t + 4], T[pm][:, 0:128], 128, 128, "s")
+        if l < 2:
+            o["otr"], o["z"] = pack(l + 1, k, o["pms"], "pt", ZQ)
+        else:
+            q = "q1" if k % 2 == 0 else "q2"
+            o["otr"] = MM([o["pms"], free[q], c_pall], [(T[q][:, 0:4, g2, :], T.pall[:, x2, g2], T.pms[:, t + 4, :, x2, :], x2 == 0, x2 == 1, 64)
+                                                        for g2 in range(2) for x2 in range(2)])
+            o["z"] = free[q] = V([o["otr"]], "tr", T.yo[:, 128 * k:128 * k + 128], T[q][:, 0:4], cy=128)
+            dma("y", [o["z"]], T.y[:, 128 * k:128 * k + 128], T.yo[:, 128 * k:128 * k + 128], "yd")
+    last = {}
+
+    def then(q, *names):
+        for t, name in names:
+            if 0 <= t < NT and name in B[t]:
+                x = B[t][name]
+                for n in (x if isinstance(x, list) else [x]):
+                    if q in n["dur"]:
+                        n["prev"] = last.get(q)
+                        last[q] = n
+
+    then("v", (0, "lt"), (0, "off"))
+    then("p", (0, "tr"), (0, "a"))
+    then("s", (0, "ls"), (0, "lt"))
+    for t in range(NT + 1):
+        steps(then, t)
+
+    order = layout(nodes)
+    total = {}
+    for n in order:
+        s = n["sem"] or n["q"]
+        total[s] = total.get(s, 0) + n["n"]
+        n["tok"] = (s, total[s])
+    waited = {}
+
+    def wait(q, s, val):
+        if waited.get((q, s), 0) < val:
+            queues[q].wait_ge(T.sem[s], val)
+            waited[(q, s)] = val
+
+    sent = 0
+    for n in order:
+        need = {}
+        for d in n["deps"]:
+            s, val = d["tok"]
+            need[s] = max(need.get(s, 0), val)
+        for s in sorted(need):
+            wait(n["q"], s, need[s])
+        x = n["emit"](n["q"])
+        if x is None:
+            sent += n["n"]
+        else:
+            x.then_inc(T.sem[n["tok"][0]], n["n"])
+    for s in sorted(total):
+        wait("y", s, total[s])
+    wait("y", "loc", sent)

@@ -6,67 +6,75 @@ COPY = ActivationFunctionType.Copy
 NBLK = 4
 NT = 3 * NBLK
 A4 = [[0], [1], [2], [3]]
-SENDS = {0: [[0, 1], [2, 3]], 1: A4, 2: A4}
-CYC, PEC, GAT, FIX, WAKE, REM, DMA = 1.0e-3, 0.5e-3, 1.56e-3, 0.05, 0.06, 4.2, 2.0
-TP, TQ = 2, 2
-GX = 0
-UNITS = [[("v", 0, 40), ("s", 40, 24)], [("v", 64, 20), ("s", 84, 44)]]
-LTQ, ZQ, LSQ = "v", "v", "s"
+MODE = "BBA"
+SENDS = {0: [[0], [1, 2, 3]], 1: A4, 2: A4}
+CYC, PEC, GAT, FIX, WAKE, REM, DMA = 1.0e-3, 0.5e-3, 1.56e-3, 0.05, 0.06, 3.5, 2.0
+TQ = 4
+NV = {"AA": 64, "AB": 60, "BA": 62, "BB": 58, "AY": 60, "BY": 58}
+EXTRA = {2: {"v": "gb"}, 3: {"v": "og", "p": "wm0"}, 4: {"s": "wc0", "p": "wm1"}, 5: {"s": "wc1"}}
+
+
+def units(m):
+    n = NV[m]
+    return [[("v", 0, 40), ("s", 40, 24)], [("v", 64, n - 40), ("s", 24 + n, 104 - n)]]
 
 
 def steps(then, t):
-    then("v", (t, "gv0"), (t - 1, "z"), (t + 1, "lt"), (t, "gv1"), (t + 1, "off"))
-    then("s", (t, "gs0"), (t - 1, "pms"), (t + 1, "ls"), (t, "gs1"))
-    then("p", (t - 1, "m1"), (t - 1, "otr"), (t + 1, "tr"), (t + 1, "a"), (t, "m0"))
+    then("v", (t, "gv0"), (t, "xv"), (t - 1, "z"), (t + 1, "lt"), (t, "gv1"), (t + 1, "off"))
+    then("s", (t, "gs0"), (t - 1, "pms"), (t, "xs"), (t, "gs1"))
+    then("p", (t - 1, "m1"), (t - 1, "otr"), (t + 1, "tr"), (t + 1, "a"), (t, "m0"), (t, "xp"))
 
 
 SCRATCH = {
     "xi": ("sbuf", [128, 512], "int32"),
     "gi": ("sbuf", [128, 3], "int32"),
+    "gd": ("dram", [4, 128, 3], "int32"),
+    "gg": ("sbuf", [128, 3], "int32"),
     "wi": ("sbuf", [128, 6], "int32"),
     "tab": ("sbuf", [128, 3, 4096], "bfloat16"),
     "jc": ("sbuf", [128, 128], "bfloat16"),
     "jl": ("sbuf", [128, 128], "bfloat16"),
+    "jr": ("sbuf", [128, 128], "bfloat16"),
     "pint": ("sbuf", [128, 4], "int32"),
-    "pc": ("sbuf", [128, 4], "float32"),
     "pf": ("sbuf", [128, 1], "float32"),
-    "pbits": ("sbuf", [128, 4], "float32"),
+    "plow": ("sbuf", [128, 1], "float32"),
     "m16": ("sbuf", [128, 16], "float32"),
-    "vc": ("sbuf", [128, 4], "float32"),
     "ident": ("sbuf", [128, 128], "bfloat16"),
     "id4": ("sbuf", [128, 4, 2, 16], "bfloat16"),
     "pall": ("sbuf", [128, 2, 2, 4, 2, 16], "bfloat16"),
     "ones": ("sbuf", [128, 128], "bfloat16"),
     "msk": ("sbuf", [128, 16, 128], "bfloat16"),
-    "gf": ("sbuf", [128, 4], "float32"),
-    "wf": ("sbuf", [128, 6], "float32"),
+    "gl": ("sbuf", [128, 3], "float32"),
+    "gbs": ("sbuf", [128, 3], "float32"),
+    "og": ("sbuf", [128, 3, 128], "bfloat16"),
     "dg": ("sbuf", [128, 3, 128], "bfloat16"),
-    "nbs": ("sbuf", [128, 2, 128], "bfloat16"),
-    "selp": ("sbuf", [128, 4, 128], "bfloat16"),
-    "sel": ("sbuf", [128, 2, 16, 128], "bfloat16"),
+    "one": ("sbuf", [128, 3, 128], "bfloat16"),
+    "wf": ("sbuf", [128, 6], "float32"),
     "oh": ("sbuf", [128, 6, 128], "bfloat16"),
     "wm": ("sbuf", [128, 3, 128], "bfloat16"),
+    "wc": ("sbuf", [128, 3, 4, 128], "bfloat16"),
     "xb": ("sbuf", [128, 512], "bfloat16"),
     "xt": ("sbuf", [128, NBLK, 4, 2, 16], "bfloat16"),
-    "ls": ("sbuf", [128, NT, 128], "bfloat16"),
+    "cu": ("sbuf", [128, 3, NBLK, 128], "bfloat16"),
     "lt": ("sbuf", [128, NT, 128], "bfloat16"),
     "off": ("sbuf", [128, NT, 128], "uint16"),
     "gt": ("sbuf", [128, NT, 2048], "bfloat16"),
-    "pms": ("sbuf", [128, NT + NBLK, 4, 2, 16], "bfloat16"),
+    "pms": ("sbuf", [128, NBLK, 4, 2, 16], "bfloat16"),
     "yo": ("sbuf", [128, 512], "float32"),
-    "q0": ("psum", [128, 8, 128], "bfloat16"),
     "q1": ("psum", [128, 16, 2, 16], "float32"),
-    "q2": ("psum", [128, 16, 2, 16], "float32"),
     "pm0": ("psum", [128, 512], "float32"),
     "pm1": ("psum", [128, 512], "float32"),
     "pa": ("psum", [128, 512], "float32"),
-    "pt": ("psum", [128, 8, 128], "bfloat16"),
+    "pw": ("psum", [128, 512], "float32"),
+    "pv": ("psum", [128, 512], "float32"),
+    "pl": ("psum", [128, 512], "float32"),
     "pr": ("psum", [128, 8, 128], "bfloat16"),
 }
-SEMAPHORES = ["v", "p", "s", "k", "x0", "x1", "x2", "x3", "gl", "wl", "t00", "t01", "t10", "t11", "t20", "t21", "yd", "loc"]
+SEMAPHORES = ["v", "p", "s", "k", "x0", "x1", "gs", "gd", "gg", "ga", "wl", "yd", "loc"]
+SEMAPHORES += ["t%d%d" % (_l, _q) for _l in range(3) for _q in range(4)]
 for _e in SENDS:
     for _c in range(len(SENDS[_e])):
-        SCRATCH["z%d_%d" % (_e, _c)] = ("sbuf", [128, 7, len(SENDS[_e][_c]), 32], "bfloat16")
+        SCRATCH["z%d_%d" % (_e, _c)] = ("sbuf", [128, 4 if MODE[_e] == "A" else 7, len(SENDS[_e][_c]), 128 if MODE[_e] == "A" else 32], "bfloat16")
         SEMAPHORES.append("a%d_%d" % (_e, _c))
 
 
@@ -148,8 +156,12 @@ def rank_program(g, core, T, topo):
             return x
         return node({"p": 0.02 + sum([c[5] for c in calls]) * PEC}, deps, emit)
 
-    def TR(deps, out, in_):
-        return node({"p": 0.02 + 128 * PEC}, deps, lambda q: g.tensor.transpose(out, in_, T.ident[:]))
+    def TR(deps, calls):
+        def emit(q):
+            for out, in_ in calls:
+                x = g.tensor.transpose(out, in_, T.ident[:])
+            return x
+        return node({"p": 0.02 + 128 * PEC * len(calls)}, deps, emit)
 
     def dma(q, deps, out, in_, s, more=0.0, pri=0.0):
         x = node({q: 0.05}, deps, lambda qq: queues[qq].dma_start(out, in_), s, 16, DMA + more)
@@ -159,38 +171,33 @@ def rank_program(g, core, T, topo):
     def iota(out, n, pattern, base, cm):
         return node({"k": 0.13 + 2 * n * CYC}, [], lambda q: g.iota(out, pattern, base, cm, allow_small_or_imprecise_dtypes=True))
 
-    d_give = [dma("s", [], T.gi[32 * c:32 * c + 32, :], T.give[32 * (r ^ c):32 * (r ^ c) + 32, :], "gl") for c in range(4)]
-    d_x = [dma("y", [], T.xi[:, 128 * h:128 * h + 128], T.x[:, 128 * h:128 * h + 128], "x%d" % h, 0.3 * h) for h in range(4)]
-    d_wire = dma("y", [], T.wi[:], T.wires[:], "wl", 1.2)
+    d_gd = dma("s", [], T.gd[0], T.give[:], "gd")
+    d_give = dma("s", [], T.gi[:], T.give[:], "gs")
+    d_x = [dma("y", [], T.xi[:, 256 * h:256 * h + 256], T.x[:, 256 * h:256 * h + 256], "x%d" % h, 0.1 * h) for h in range(2)]
+    d_wire = dma("s", [], T.wi[:], T.wires[:], "wl")
     tabs = [[], [], []]
 
     def load_table(l, h, n, more, deps=()):
         tabs[l].append(dma("y", list(deps), T.tab[16 * h:16 * h + 16 * n, l, :], T.tb[h:h + n, l * 65536:(l + 1) * 65536],
-                           "t%d%d" % (l, h // n % 2), more, -1000.0))
+                           "t%d%d" % (l, h // n % 4), more, -1000.0))
 
-    load_table(0, 0, 4, 2.5)
-    load_table(0, 4, 4, 4.5)
+    for h in (0, 2, 4):
+        load_table(0, h, 2, 1.5 + 0.4 * h)
 
     s0 = 32 if r % 2 == 0 else -32
     s1 = 64 if r < 2 else -64
     k_pint = node({"k": 0.13}, [], lambda q: g.iota(T.pint[:, 0:1], [[0, 1]], 0, 1))
-    k_pc = iota(T.pc[:, 0:3], 3, [[16, 3]], -15, 1)
     k_pf = iota(T.pf[:], 1, [[0, 1]], 0, 1)
     k_jc = iota(T.jc[:], 128, [[1, 128]], 0, 0)
     k_jl = iota(T.jl[:], 128, [[-s1, 2], [-s0, 2], [1, 32]], 32 * (r ^ 3), 0)
-    c_ones = V([], "set", T.ones[:], 1.0)
+    k_jr = iota(T.jr[:], 128, [[s1, 2], [s0, 2], [1, 32]], 32 * r, 0)
     c_pz = V([], "set", T.pall[:], 0.0, cy=256)
-    c_hi = V([k_pint], "ts", T.pint[:, 1:2], T.pint[:, 0:1], 4, 1, OP.arith_shift_right, OP.bitwise_and)
+    c_ones = V([], "set", T.ones[:], 1.0)
     c_lo = V([k_pint], "ts", T.pint[:, 2:3], T.pint[:, 0:1], 15, None, OP.bitwise_and)
-    c_bits = V([c_hi, c_lo], "copy", T.pbits[:, 0:2], T.pint[:, 1:3])
-    bit, low = T.pbits[:, 0:1], T.pbits[:, 1:2]
-    c_vc = [V([c_bits, k_pc], "ts", T.vc[:, 0:1], bit, 0.0, T.pc[:, 1:2], OP.is_equal, OP.mult),
-            V([c_bits, k_pc], "ts", T.vc[:, 1:2], bit, 0.0, T.pc[:, 2:3], OP.is_equal, OP.mult),
-            V([c_bits, k_pc], "ts", T.vc[:, 2:3], bit, T.pc[:, 0:1], None, OP.mult),
-            V([c_bits, k_pc], "ts", T.vc[:, 3:4], bit, T.pc[:, 1:2], None, OP.mult)]
+    c_low = V([c_lo], "copy", T.plow[:], T.pint[:, 2:3])
     c_id = V([k_jc, k_pf], "ts", T.ident[:], T.jc[:], T.pf[:], None, OP.is_equal)
     c_id4 = V([k_jc, k_pf], "ts", T.id4[:], T.jc[:], T.pf[:], None, OP.is_equal)
-    c_m16 = V([k_jc, c_bits], "ts", T.m16[:], T.jc[:, 0:16], low, None, OP.is_equal)
+    c_m16 = V([k_jc, c_low], "ts", T.m16[:], T.jc[:, 0:16], T.plow[:], None, OP.is_equal)
     c_pall = []
     for x2 in range(2):
         for g2 in range(2):
@@ -223,94 +230,123 @@ def rank_program(g, core, T, topo):
             return None
         return node({"k": 0.6}, deps, emit, name, total_eng, REM - 0.6)
 
-    c_gf = V([d_give], "ts", T.gf[:, 0:3], T.gi[:], 1.0, None, OP.add)
-    c_d = [scaled([c_gf, c_ones], T.dg[:, l, :], T.ones[:], T.gf[:, l:l + 1]) for l in range(3)]
-    m_nb0 = TR([c_d[0], c_id], T.pr[:, 0, :], T.dg[:, 0, :])
+    arr, own = {}, {}
+    free = {"pr": None, "pl": None, "pw": None, "pv": None, "pa": None, "pm0": None, "pm1": None, "q1": None}
+    a_give = send([d_gd], "ga", lambda d: T.gd[0], lambda d: T.gd[d])
+
     xt = []
     for k in range(NBLK):
-        a = V([d_x[k]], "copy", T.xb[:, 128 * k:128 * k + 128], T.xi[:, 128 * k:128 * k + 128], cy=128)
+        a = V([d_x[k // 2]], "copy", T.xb[:, 128 * k:128 * k + 128], T.xi[:, 128 * k:128 * k + 128], cy=128)
         xt.append(V([a], "tr", T.xt[:, k], T.xb[:, 128 * k:128 * k + 128]))
-    c_selp = [V([m_nb0, c_vc[v]], "ts", T.selp[:, v, :], T.pr[:, 0, :], T.vc[:, v:v + 1], None, OP.is_equal) for v in range(4)]
-    PV = [(0, 0), (0, 1), (1, 0), (1, 1)]
-    arr, zt = {}, {}
-    free = {"pt": None, "pr": c_selp, "q1": None, "q2": None}
+
+    c_one = {}
+    c_gl = V([d_give], "copy", T.gl[:], T.gi[:])
+    for e in range(3):
+        if MODE[e] == "B":
+            a = V([c_gl, k_jr, k_pf], "ts", T.dg[:, e, :], T.jr[:], T.pf[:], T.gl[:, e:e + 1], OP.is_equal, OP.mult)
+            a = MM([a, c_ones, free["pw"]], [(T.pw[:, 0:128], T.ones[:], T.dg[:, e, :], True, True, 128)])
+            free["pw"] = c_one[e] = V([a, k_pf], "ts", T.one[:, e, :], T.pw[:, 0:128], T.pf[:], None, OP.is_equal, cy=128)
 
     def zslot(e, k):
         for ci, blks in enumerate(SENDS[e]):
             if k in blks:
-                return ci, blks.index(k), blks
+                return T["z%d_%d" % (e, ci)], "a%d_%d" % (e, ci), blks.index(k), blks
 
-    def pack(e, k, dep, bank, on):
-        ci, i, blks = zslot(e, k)
-        z = T["z%d_%d" % (e, ci)]
-        a = TR([dep, c_id] + [free[bank]], T[bank][:, 0, :], T.pms[:, 4 * e + k])
-        free[bank] = zt[(e, k)] = VS([a], z[:, 3:7, i, :], T[bank][:, 0, :], 64, 128, on)
+    def post(e, k, deps, src, on, o=None):
+        z, name, i, blks = zslot(e, k)
+        if MODE[e] == "A":
+            own[(e, k)] = c = VS(deps, z[:, 3, i, :], src, 128, 128, on)
+        else:
+            c = VS(deps, T.cu[:, e, k, :], src, 128, 128, on)
+            a = MM([c, c_one[e], free["pl"]], [(T.pl[:, 0:128], T.cu[:, e, k, :], T.one[:, e, :], True, True, 128)])
+            free["pl"] = own[(e, k)] = VS([a], z[:, 3:7, i, :], T.pl[:, 0:128], 128, 128, "v" if o is not None else "vs")
+            if o is not None:
+                o["otr"], o["z"] = a, own[(e, k)]
         if k == blks[-1]:
-            c = send([zt[(e, b)] for b in blks], "a%d_%d" % (e, ci), lambda d: z[:, 3 + d, :, :], lambda d: z[:, 3 - d, :, :])
+            n = send([own[(e, b)] for b in blks], name, lambda d: z[:, 3 if MODE[e] == "A" else 3 + d, :, :], lambda d: z[:, 3 - d, :, :])
             for b in blks:
-                arr[(e, b)] = c
-        return a, zt[(e, k)]
+                arr[(e, b)] = n
+        return c
 
     for k in range(NBLK):
-        q = "q1" if k % 2 == 0 else "q2"
-        a = MM([xt[k], c_selp, free[q]], [(T[q][:, 0:4, bp, :], T.selp[:, 2 * bp + g2, :], T.xt[:, k, :, g2, :], g2 == 0, g2 == 1, 64)
-                                          for bp, g2 in PV])
-        free[q] = VS([a], T.pms[:, k], T[q][:, 0:4], 128, 128)
-        pack(0, k, free[q], "pt" if k % 2 == 0 else "pr", "vs")
+        a = MM([xt[k], c_pall, free["q1"]], [(T.q1[:, 0:4, bp, :], T.pall[:, g2, bp], T.xt[:, k, :, g2, :], g2 == 0, g2 == 1, 64)
+                                             for bp in range(2) for g2 in range(2)])
+        free["q1"] = post(0, k, [a], T.q1[:, 0:4], "vs")
+    load_table(0, 6, 2, 2.5, [own[(0, 1)]])
 
-    m_nb = [TR([c_d[l], c_id], T.q0[:, l, :], T.dg[:, l, :]) for l in (1, 2)]
+    X = {}
+    d_gg = [dma("y", [a_give if j < 3 else None], T.gg[32 * j:32 * j + 32, :],
+                T.gd[3 - j, 32 * r:32 * r + 32, :] if j < 3 else T.give[32 * r:32 * r + 32, :], "gg", 0.0, -500.0) for j in (3, 0, 1, 2)]
+    c_gb = X["gb"] = V([d_gg], "copy", T.gbs[:], T.gg[:])
     c_wf = V([d_wire], "copy", T.wf[:], T.wi[:])
     c_w = []
     for l in range(3):
-        bank = [T.pa, T.pm0, T.pm1][l]
         o0 = V([c_wf, k_jl], "ts", T.oh[:, 2 * l, :], T.jl[:], T.wf[:, 2 * l:2 * l + 1], 64.0, OP.is_equal, OP.mult)
         o1 = V([c_wf, k_jl], "ts", T.oh[:, 2 * l + 1, :], T.jl[:], T.wf[:, 2 * l + 1:2 * l + 2], None, OP.is_equal)
-        a = MM([o0, o1, c_id], [(bank[:, 0:128], T.oh[:, 2 * l, :], T.ident[:], True, False, 128),
-                                (bank[:, 0:128], T.oh[:, 2 * l + 1, :], T.ident[:], False, True, 128)])
-        c_w.append(VS([a], T.wm[:, l, :], bank[:, 0:128], 128, 128))
-    c_one = [V([m_nb, k_pc], "ts", T.nbs[:, l, :], T.q0[:, l + 1, :], T.pc[:, 1:2], None, OP.is_equal) for l in range(2)]
-    c_sel = [[scaled([c_one[l], c_m16], T.sel[:, l, u, :], T.nbs[:, l, :], T.m16[:, u:u + 1]) for u in range(16)] for l in range(2)]
+        b = ["pm1", "pm0", "pa"][l]
+        a = MM([o0, o1, c_id, free[b]], [(T[b][:, 0:128], T.oh[:, 2 * l, :], T.ident[:], True, False, 128),
+                                         (T[b][:, 0:128], T.oh[:, 2 * l + 1, :], T.ident[:], False, True, 128)])
+        free[b] = c_wm = VS([a], T.wm[:, l, :], T[b][:, 0:128], 128, 128)
+        if MODE[l] == "B":
+            c_w.append([c_wm])
+            continue
+        c_og = X["og"] = V([c_gb, k_jc], "ts", T.og[:, l, :], T.jc[:], T.gbs[:, l:l + 1], None, OP.is_equal)
+        c_w.append([])
+        for h in range(2):
+            b = ["pw", "pv"][h]
+            X["wm%d" % h] = []
+            a = free[b]
+            for e, j in enumerate((2 * h, 2 * h + 1)):
+                a = MM([c_wm, c_og, a], [(T[b][:, 128 * e:128 * e + 128], T.og[32 * j:32 * j + 32, l, :], T.wm[32 * j:32 * j + 32, l, :], True, True, 128)])
+                X["wm%d" % h].append(a)
+            free[b] = X["wc%d" % h] = VS([a], T.wc[:, l, 2 * h:2 * h + 2, :], T[b][:, 0:256], 256, 256, "s")
+            c_w[l].append(free[b])
     c_msk = [scaled([c_m16, c_id], T.msk[:, u, :], T.ident[:], T.m16[:, u:u + 1]) for u in range(16)]
 
-    free.update({"pa": c_w[0], "pm0": c_w[1], "pm1": c_w[2]})
     B = []
     for t in range(NT):
         l, k = divmod(t, NBLK)
         pm = "pm%d" % (t % 2)
         o = {}
         B.append(o)
-        ci, i, blks = zslot(l, k)
-        z = T["z%d_%d" % (l, ci)]
-        if len(blks) > 1:
-            c = o["ls"] = VS([arr[(l, k)], zt[(l, k)]], T.ls[:, t, :], z[:, 0:4, i, :], 64, 128, LSQ)
-            o["tr"] = TR([c, free["pr"], c_id], T.pr[:, 0, :], T.ls[:, t, :])
+        for q, n in EXTRA.get(t, {}).items():
+            o["x" + q] = X[n]
+        z, _, i, blks = zslot(l, k)
+        if MODE[l] == "A":
+            o["a"] = MM([arr[(l, k)], own[(l, k)], c_w[l], free["pa"]],
+                        [(T.pa[:, 0:128], T.wc[:, l, j, :], z[:, j, i, :], j == 3, j == 2, 128) for j in (3, 0, 1, 2)])
         else:
-            o["tr"] = TR([arr[(l, k)], zt[(l, k)], free["pr"], c_id], T.pr[:, 0, :], z[:, 0:4, 0, :])
-        o["lt"] = free["pr"] = VS([o["tr"]], T.lt[:, t, :], T.pr[:, 0, :], 64, 128, LTQ)
-        o["a"] = MM([o["lt"], c_w[l], free["pa"]], [(T.pa[:, 0:128], T.wm[:, l, :], T.lt[:, t, :], True, True, 128)])
+            o["tr"] = TR([arr[(l, k)], own[(l, k)], free["pr"], c_id],
+                         [(T.pr[:, 0, :], z[:, 0:4, 0, :])] if len(blks) == 1 else [(T.pr[32 * j:32 * j + 32, 0, :], z[:, j, i, :]) for j in range(4)])
+            o["lt"] = free["pr"] = VS([o["tr"]], T.lt[:, t, :], T.pr[:, 0, :], 64, 128, "v")
+            o["a"] = MM([o["lt"], c_w[l], free["pa"]], [(T.pa[:, 0:128], T.wm[:, l, :], T.lt[:, t, :], True, True, 128)])
         o["off"] = free["pa"] = V([o["a"]], "copy", T.off[:, t, :], T.pa[:, 0:128], cy=128)
         if t == 0:
             for l2 in (1, 2):
-                for h in range(0, 8, TP):
-                    load_table(l2, h, TP, 0.6, [arr[(0, GX)] if l2 == 1 and h < TP * TQ else (tabs[1] + tabs[2])[-TQ]])
-        lhs = [T.msk[:, u, :] if l == 2 else T.sel[:, l, u, :] for u in range(16)]
+                for h in range(8):
+                    load_table(l2, h, 1, 0.6, [arr[(0, 0)] if l2 == 1 and h < TQ else (tabs[1] + tabs[2])[-TQ]])
+
+        def gather(q, b, n):
+            x = VS([o["off"], tabs[l]], T.gt[:, t, 16 * b:16 * b + 16 * n], T.tab[:, l, :].indirect(T.off[:, t, b:b + n]),
+                   16 * n * GAT / CYC, 16 * n * GAT / CYC, q)
+            j = 1 if "g%s0" % q in o else 0
+            o["g%s%d" % (q, j)] = x
+            return x
+
+        ms = []
         for h in range(2):
-            gs = []
-            for q, b, n in UNITS[h]:
-                gs.append(VS([o["off"], tabs[l]], T.gt[:, t, 16 * b:16 * b + 16 * n], T.tab[:, l, :].indirect(T.off[:, t, b:b + n]),
-                             16 * n * GAT / CYC, 16 * n * GAT / CYC, q))
-                o.setdefault("g%s%d" % (q, h), []).append(gs[-1])
-            o["m%d" % h] = MM([gs, free[pm], c_msk if l == 2 else c_sel[l]],
-                              [(T[pm][:, 64 * h:64 * h + 64], lhs[u], T.gt[:, t, 1024 * h + u:1024 * h + 1024:16], u == 0, u == 15, 64)
+            gs = [gather(q, b, n) for q, b, n in units(MODE[l] + (MODE + "Y")[l + 1])[h]]
+            o["m%d" % h] = MM([gs, free[pm], c_msk],
+                              [(T[pm][:, 64 * h:64 * h + 64], T.msk[:, u, :], T.gt[:, t, 1024 * h + u:1024 * h + 1024:16], u == 0, u == 15, 64)
                                for u in range(16)])
-        o["pms"] = free[pm] = VS([o["m0"], o["m1"]], T.pms[:, t + 4], T[pm][:, 0:128], 128, 128, "s")
+            ms.append(o["m%d" % h])
         if l < 2:
-            o["otr"], o["z"] = pack(l + 1, k, o["pms"], "pt", ZQ)
+            o["pms"] = free[pm] = post(l + 1, k, ms, T[pm][:, 0:128], "s", o)
         else:
-            q = "q1" if k % 2 == 0 else "q2"
-            o["otr"] = MM([o["pms"], free[q], c_pall], [(T[q][:, 0:4, g2, :], T.pall[:, x2, g2], T.pms[:, t + 4, :, x2, :], x2 == 0, x2 == 1, 64)
-                                                        for g2 in range(2) for x2 in range(2)])
-            o["z"] = free[q] = V([o["otr"]], "tr", T.yo[:, 128 * k:128 * k + 128], T[q][:, 0:4], cy=128)
+            o["pms"] = free[pm] = VS(ms, T.pms[:, k], T[pm][:, 0:128], 128, 128, "s")
+            o["otr"] = MM([o["pms"], free["q1"], c_pall], [(T.q1[:, 0:4, g2, :], T.pall[:, x2, g2], T.pms[:, k, :, x2, :], x2 == 0, x2 == 1, 64)
+                                                           for g2 in range(2) for x2 in range(2)])
+            o["z"] = free["q1"] = V([o["otr"]], "tr", T.yo[:, 128 * k:128 * k + 128], T.q1[:, 0:4], cy=128)
             dma("y", [o["z"]], T.y[:, 128 * k:128 * k + 128], T.yo[:, 128 * k:128 * k + 128], "yd")
     last = {}
 
@@ -325,7 +361,6 @@ def rank_program(g, core, T, topo):
 
     then("v", (0, "lt"), (0, "off"))
     then("p", (0, "tr"), (0, "a"))
-    then("s", (0, "ls"), (0, "lt"))
     for t in range(NT + 1):
         steps(then, t)
 

@@ -6,23 +6,28 @@ COPY = ActivationFunctionType.Copy
 NBLK = 4
 NT = 3 * NBLK
 A4 = [[0], [1], [2], [3]]
-MODE = "BBA"
+MODE = "BAA"
 SENDS = {0: [[0], [1, 2, 3]], 1: A4, 2: A4}
 CYC, PEC, GAT, FIX, WAKE, REM, DMA = 1.0e-3, 0.5e-3, 1.56e-3, 0.05, 0.06, 3.5, 2.0
-TQ = 4
-NV = {"AA": 64, "AB": 60, "BA": 62, "BB": 58, "AY": 60, "BY": 58}
-EXTRA = {2: {"v": "gb"}, 3: {"v": "og", "p": "wm0"}, 4: {"s": "wc0", "p": "wm1"}, 5: {"s": "wc1"}}
+TQ = {1: 4, 2: 3}
+NV = [54, 50, 60, 64, 58, 56, 62, 60, 50, 54, 56]
+V0 = [44, 40, 42, 50, 48, 52, 54, 46, 40, 50, 50]
+EXTRA = {1: {"v": ["gb", "og1"]}, 2: {"v": ["og2"], "p": ["wm1"]}, 3: {"s": ["wc1"]}, 4: {"p": ["wm2"]}, 6: {"s": ["wc2"]}}
 
 
-def units(m):
-    n = NV[m]
-    return [[("v", 0, 40), ("s", 40, 24)], [("v", 64, n - 40), ("s", 24 + n, 104 - n)]]
+def pieces(t):
+    if t == NT - 1:
+        return [(0, 64, [("v", 0, 42), ("s", 42, 22)]), (64, 64, [("v", 64, 28), ("s", 92, 36)])]
+    n = NV[t]
+    return [(0, n, [("v", 0, V0[t]), ("v", V0[t], n - V0[t])]), (n, 128 - n, [("s", n, 128 - n)])]
 
 
 def steps(then, t):
-    then("v", (t, "gv0"), (t, "xv"), (t - 1, "z"), (t + 1, "lt"), (t, "gv1"), (t + 1, "off"))
-    then("s", (t, "gs0"), (t - 1, "pms"), (t, "xs"), (t, "gs1"))
-    then("p", (t - 1, "m1"), (t - 1, "otr"), (t + 1, "tr"), (t + 1, "a"), (t, "m0"), (t, "xp"))
+    early = [(t + 1, "lt")] if t == 0 else []
+    then("v", (t, "gv0"), (t, "xv"), (t - 1, "pms"), *early, (t, "gv1"), (t + 1, "off"), (t - 1, "z"), (t + 2, "lt"))
+    then("s", (t, "xs"), (t, "gs0"), (t, "gs1"))
+    early = [(t + 1, "tr")] if t == 0 else []
+    then("p", (t - 1, "m1"), *early, (t + 1, "a"), (t + 2, "tr"), (t, "xp"), (t - 1, "otr"), (t, "m0"))
 
 
 SCRATCH = {
@@ -47,15 +52,15 @@ SCRATCH = {
     "gl": ("sbuf", [128, 3], "float32"),
     "gbs": ("sbuf", [128, 3], "float32"),
     "og": ("sbuf", [128, 3, 128], "bfloat16"),
-    "dg": ("sbuf", [128, 3, 128], "bfloat16"),
-    "one": ("sbuf", [128, 3, 128], "bfloat16"),
+    "dg": ("sbuf", [128, 128], "bfloat16"),
+    "one": ("sbuf", [128, 128], "bfloat16"),
     "wf": ("sbuf", [128, 6], "float32"),
     "oh": ("sbuf", [128, 6, 128], "bfloat16"),
     "wm": ("sbuf", [128, 3, 128], "bfloat16"),
     "wc": ("sbuf", [128, 3, 4, 128], "bfloat16"),
     "xb": ("sbuf", [128, 512], "bfloat16"),
     "xt": ("sbuf", [128, NBLK, 4, 2, 16], "bfloat16"),
-    "cu": ("sbuf", [128, 3, NBLK, 128], "bfloat16"),
+    "cu": ("sbuf", [128, NBLK, 128], "bfloat16"),
     "lt": ("sbuf", [128, NT, 128], "bfloat16"),
     "off": ("sbuf", [128, NT, 128], "uint16"),
     "gt": ("sbuf", [128, NT, 2048], "bfloat16"),
@@ -234,34 +239,29 @@ def rank_program(g, core, T, topo):
     free = {"pr": None, "pl": None, "pw": None, "pv": None, "pa": None, "pm0": None, "pm1": None, "q1": None}
     a_give = send([d_gd], "ga", lambda d: T.gd[0], lambda d: T.gd[d])
 
-    xt = []
+    xb, xt = [], []
     for k in range(NBLK):
-        a = V([d_x[k // 2]], "copy", T.xb[:, 128 * k:128 * k + 128], T.xi[:, 128 * k:128 * k + 128], cy=128)
-        xt.append(V([a], "tr", T.xt[:, k], T.xb[:, 128 * k:128 * k + 128]))
+        xb.append(V([d_x[k // 2]], "copy", T.xb[:, 128 * k:128 * k + 128], T.xi[:, 128 * k:128 * k + 128], cy=128))
+        xt.append(V([xb[k]], "tr", T.xt[:, k], T.xb[:, 128 * k:128 * k + 128]))
 
-    c_one = {}
     c_gl = V([d_give], "copy", T.gl[:], T.gi[:])
-    for e in range(3):
-        if MODE[e] == "B":
-            a = V([c_gl, k_jr, k_pf], "ts", T.dg[:, e, :], T.jr[:], T.pf[:], T.gl[:, e:e + 1], OP.is_equal, OP.mult)
-            a = MM([a, c_ones, free["pw"]], [(T.pw[:, 0:128], T.ones[:], T.dg[:, e, :], True, True, 128)])
-            free["pw"] = c_one[e] = V([a, k_pf], "ts", T.one[:, e, :], T.pw[:, 0:128], T.pf[:], None, OP.is_equal, cy=128)
+    c_dg = V([c_gl, k_jr, k_pf], "ts", T.dg[:], T.jr[:], T.pf[:], T.gl[:, 0:1], OP.is_equal, OP.mult)
+    a = MM([c_dg, c_ones], [(T.pw[:, 0:128], T.ones[:], T.dg[:], True, True, 128)])
+    free["pw"] = c_one = V([a, k_pf], "ts", T.one[:], T.pw[:, 0:128], T.pf[:], None, OP.is_equal, cy=128)
 
     def zslot(e, k):
         for ci, blks in enumerate(SENDS[e]):
             if k in blks:
                 return T["z%d_%d" % (e, ci)], "a%d_%d" % (e, ci), blks.index(k), blks
 
-    def post(e, k, deps, src, on, o=None):
+    def post(e, k, deps, src, on):
         z, name, i, blks = zslot(e, k)
         if MODE[e] == "A":
             own[(e, k)] = c = VS(deps, z[:, 3, i, :], src, 128, 128, on)
         else:
-            c = VS(deps, T.cu[:, e, k, :], src, 128, 128, on)
-            a = MM([c, c_one[e], free["pl"]], [(T.pl[:, 0:128], T.cu[:, e, k, :], T.one[:, e, :], True, True, 128)])
-            free["pl"] = own[(e, k)] = VS([a], z[:, 3:7, i, :], T.pl[:, 0:128], 128, 128, "v" if o is not None else "vs")
-            if o is not None:
-                o["otr"], o["z"] = a, own[(e, k)]
+            c = VS(deps, T.cu[:, k, :], src, 128, 128, on)
+            a = MM([c, c_one, free["pl"]], [(T.pl[:, 0:128], T.cu[:, k, :], T.one[:], True, True, 128)])
+            free["pl"] = own[(e, k)] = VS([a], z[:, 3:7, i, :], T.pl[:, 0:128], 128, 128)
         if k == blks[-1]:
             n = send([own[(e, b)] for b in blks], name, lambda d: z[:, 3 if MODE[e] == "A" else 3 + d, :, :], lambda d: z[:, 3 - d, :, :])
             for b in blks:
@@ -271,7 +271,7 @@ def rank_program(g, core, T, topo):
     for k in range(NBLK):
         a = MM([xt[k], c_pall, free["q1"]], [(T.q1[:, 0:4, bp, :], T.pall[:, g2, bp], T.xt[:, k, :, g2, :], g2 == 0, g2 == 1, 64)
                                              for bp in range(2) for g2 in range(2)])
-        free["q1"] = post(0, k, [a], T.q1[:, 0:4], "vs")
+        free["q1"] = post(0, k, [a], T.q1[:, 0:4], "s" if k == 0 else "vs")
     load_table(0, 6, 2, 2.5, [own[(0, 1)]])
 
     X = {}
@@ -290,17 +290,15 @@ def rank_program(g, core, T, topo):
         if MODE[l] == "B":
             c_w.append([c_wm])
             continue
-        c_og = X["og"] = V([c_gb, k_jc], "ts", T.og[:, l, :], T.jc[:], T.gbs[:, l:l + 1], None, OP.is_equal)
-        c_w.append([])
-        for h in range(2):
-            b = ["pw", "pv"][h]
-            X["wm%d" % h] = []
-            a = free[b]
-            for e, j in enumerate((2 * h, 2 * h + 1)):
-                a = MM([c_wm, c_og, a], [(T[b][:, 128 * e:128 * e + 128], T.og[32 * j:32 * j + 32, l, :], T.wm[32 * j:32 * j + 32, l, :], True, True, 128)])
-                X["wm%d" % h].append(a)
-            free[b] = X["wc%d" % h] = VS([a], T.wc[:, l, 2 * h:2 * h + 2, :], T[b][:, 0:256], 256, 256, "s")
-            c_w[l].append(free[b])
+        c_og = X["og%d" % l] = V([c_gb, k_jc], "ts", T.og[:, l, :], T.jc[:], T.gbs[:, l:l + 1], None, OP.is_equal)
+        b = ["pw", "pv"][l % 2]
+        X["wm%d" % l] = []
+        a = free[b]
+        for j in range(4):
+            a = MM([c_wm, c_og, a], [(T[b][:, 128 * j:128 * j + 128], T.og[32 * j:32 * j + 32, l, :], T.wm[32 * j:32 * j + 32, l, :], True, True, 128)])
+            X["wm%d" % l].append(a)
+        free[b] = X["wc%d" % l] = VS([a], T.wc[:, l, :, :], T[b][:, 0:512], 512, 512, "s")
+        c_w.append([free[b]])
     c_msk = [scaled([c_m16, c_id], T.msk[:, u, :], T.ident[:], T.m16[:, u:u + 1]) for u in range(16)]
 
     B = []
@@ -309,8 +307,10 @@ def rank_program(g, core, T, topo):
         pm = "pm%d" % (t % 2)
         o = {}
         B.append(o)
-        for q, n in EXTRA.get(t, {}).items():
-            o["x" + q] = X[n]
+        for q in EXTRA.get(t, {}):
+            o["x" + q] = []
+            for n in EXTRA[t][q]:
+                o["x" + q] += X[n] if isinstance(X[n], list) else [X[n]]
         z, _, i, blks = zslot(l, k)
         if MODE[l] == "A":
             o["a"] = MM([arr[(l, k)], own[(l, k)], c_w[l], free["pa"]],
@@ -324,7 +324,7 @@ def rank_program(g, core, T, topo):
         if t == 0:
             for l2 in (1, 2):
                 for h in range(8):
-                    load_table(l2, h, 1, 0.6, [arr[(0, 0)] if l2 == 1 and h < TQ else (tabs[1] + tabs[2])[-TQ]])
+                    load_table(l2, h, 1, 0.6, [arr[(0, 0)] if l2 == 1 and h < TQ[1] else (tabs[1] + tabs[2])[-TQ[l2]]])
 
         def gather(q, b, n):
             x = VS([o["off"], tabs[l]], T.gt[:, t, 16 * b:16 * b + 16 * n], T.tab[:, l, :].indirect(T.off[:, t, b:b + n]),
@@ -334,16 +334,16 @@ def rank_program(g, core, T, topo):
             return x
 
         ms = []
-        for h in range(2):
-            gs = [gather(q, b, n) for q, b, n in units(MODE[l] + (MODE + "Y")[l + 1])[h]]
+        for h, (lo, w, calls) in enumerate(pieces(t)):
+            gs = [gather(q, b, n) for q, b, n in calls]
             o["m%d" % h] = MM([gs, free[pm], c_msk],
-                              [(T[pm][:, 64 * h:64 * h + 64], T.msk[:, u, :], T.gt[:, t, 1024 * h + u:1024 * h + 1024:16], u == 0, u == 15, 64)
+                              [(T[pm][:, lo:lo + w], T.msk[:, u, :], T.gt[:, t, 16 * lo + u:16 * lo + 16 * w:16], u == 0, u == 15, max(64, w))
                                for u in range(16)])
             ms.append(o["m%d" % h])
         if l < 2:
-            o["pms"] = free[pm] = post(l + 1, k, ms, T[pm][:, 0:128], "s", o)
+            o["pms"] = free[pm] = post(l + 1, k, ms, T[pm][:, 0:128], "v")
         else:
-            o["pms"] = free[pm] = VS(ms, T.pms[:, k], T[pm][:, 0:128], 128, 128, "s")
+            o["pms"] = free[pm] = VS(ms, T.pms[:, k], T[pm][:, 0:128], 128, 128, "v")
             o["otr"] = MM([o["pms"], free["q1"], c_pall], [(T.q1[:, 0:4, g2, :], T.pall[:, x2, g2], T.pms[:, k, :, x2, :], x2 == 0, x2 == 1, 64)
                                                            for g2 in range(2) for x2 in range(2)])
             o["z"] = free["q1"] = V([o["otr"]], "tr", T.yo[:, 128 * k:128 * k + 128], T.q1[:, 0:4], cy=128)
@@ -359,6 +359,11 @@ def rank_program(g, core, T, topo):
                         n["prev"] = last.get(q)
                         last[q] = n
 
+    way = [c_gl, xb[0], c_dg, xt[0], c_one, xb[1]]
+    for n, p in zip(way[1:], way):
+        n["prev"] = p
+    for n in c_msk:
+        n["prev"] = own[(0, 0)]
     then("v", (0, "lt"), (0, "off"))
     then("p", (0, "tr"), (0, "a"))
     for t in range(NT + 1):

from concourse.bass import DstId, RemoteDMATransfer
from concourse.mybir import AluOpType, ActivationFunctionType

OP = AluOpType
COPY = ActivationFunctionType.Copy
NBLK = 4
NT = 3 * NBLK
A4 = [[0], [1], [2], [3]]
MODE = "BAA"
SENDS = {0: [[0], [1, 2, 3]], 1: A4, 2: A4}
CYC, PEC, GAT, FIX, WAKE, REM, DMA = 1.0e-3, 0.5e-3, 1.56e-3, 0.05, 0.06, 3.5, 2.0
TQ = {1: 4, 2: 3}
NV = [54, 50, 60, 64, 58, 56, 62, 60, 50, 54, 56]
V0 = [44, 40, 42, 50, 48, 52, 54, 46, 40, 50, 50]
EXTRA = {1: {"v": ["gb", "og1"]}, 2: {"v": ["og2"], "p": ["wm1"]}, 3: {"s": ["wc1"]}, 4: {"p": ["wm2"]}, 6: {"s": ["wc2"]}}


def pieces(t):
    if t == NT - 1:
        return [(0, 64, [("v", 0, 42), ("s", 42, 22)]), (64, 64, [("v", 64, 28), ("s", 92, 36)])]
    n = NV[t]
    return [(0, n, [("v", 0, V0[t]), ("v", V0[t], n - V0[t])]), (n, 128 - n, [("s", n, 128 - n)])]


def steps(then, t):
    early = [(t + 1, "lt")] if t == 0 else []
    then("v", (t, "gv0"), (t, "xv"), (t - 1, "pms"), *early, (t, "gv1"), (t + 1, "off"), (t - 1, "z"), (t + 2, "lt"))
    then("s", (t, "xs"), (t, "gs0"), (t, "gs1"))
    early = [(t + 1, "tr")] if t == 0 else []
    then("p", (t - 1, "m1"), *early, (t + 1, "a"), (t + 2, "tr"), (t, "xp"), (t - 1, "otr"), (t, "m0"))


SCRATCH = {
    "xi": ("sbuf", [128, 512], "int32"),
    "gi": ("sbuf", [128, 3], "int32"),
    "gd": ("dram", [4, 128, 3], "int32"),
    "gg": ("sbuf", [128, 3], "int32"),
    "wi": ("sbuf", [128, 6], "int32"),
    "tab": ("sbuf", [128, 3, 4096], "bfloat16"),
    "jc": ("sbuf", [128, 128], "bfloat16"),
    "jl": ("sbuf", [128, 128], "bfloat16"),
    "jr": ("sbuf", [128, 128], "bfloat16"),
    "pint": ("sbuf", [128, 4], "int32"),
    "pf": ("sbuf", [128, 1], "float32"),
    "plow": ("sbuf", [128, 1], "float32"),
    "m16": ("sbuf", [128, 16], "float32"),
    "ident": ("sbuf", [128, 128], "bfloat16"),
    "id4": ("sbuf", [128, 4, 2, 16], "bfloat16"),
    "pall": ("sbuf", [128, 2, 2, 4, 2, 16], "bfloat16"),
    "ones": ("sbuf", [128, 128], "bfloat16"),
    "msk": ("sbuf", [128, 16, 128], "bfloat16"),
    "gl": ("sbuf", [128, 3], "float32"),
    "gbs": ("sbuf", [128, 3], "float32"),
    "og": ("sbuf", [128, 3, 128], "bfloat16"),
    "dg": ("sbuf", [128, 128], "bfloat16"),
    "one": ("sbuf", [128, 128], "bfloat16"),
    "wf": ("sbuf", [128, 6], "float32"),
    "oh": ("sbuf", [128, 6, 128], "bfloat16"),
    "wm": ("sbuf", [128, 3, 128], "bfloat16"),
    "wc": ("sbuf", [128, 3, 4, 128], "bfloat16"),
    "xb": ("sbuf", [128, 512], "bfloat16"),
    "xt": ("sbuf", [128, NBLK, 4, 2, 16], "bfloat16"),
    "cu": ("sbuf", [128, NBLK, 128], "bfloat16"),
    "lt": ("sbuf", [128, NT, 128], "bfloat16"),
    "off": ("sbuf", [128, NT, 128], "uint16"),
    "gt": ("sbuf", [128, NT, 2048], "bfloat16"),
    "pms": ("sbuf", [128, NBLK, 4, 2, 16], "bfloat16"),
    "yo": ("sbuf", [128, 512], "float32"),
    "q1": ("psum", [128, 16, 2, 16], "float32"),
    "pm0": ("psum", [128, 512], "float32"),
    "pm1": ("psum", [128, 512], "float32"),
    "pa": ("psum", [128, 512], "float32"),
    "pw": ("psum", [128, 512], "float32"),
    "pv": ("psum", [128, 512], "float32"),
    "pl": ("psum", [128, 512], "float32"),
    "pr": ("psum", [128, 8, 128], "bfloat16"),
}
SEMAPHORES = ["v", "p", "s", "k", "x0", "x1", "gs", "gd", "gg", "ga", "wl", "yd", "loc"]
SEMAPHORES += ["t%d%d" % (_l, _q) for _l in range(3) for _q in range(4)]
for _e in SENDS:
    for _c in range(len(SENDS[_e])):
        SCRATCH["z%d_%d" % (_e, _c)] = ("sbuf", [128, 4 if MODE[_e] == "A" else 7, len(SENDS[_e][_c]), 128 if MODE[_e] == "A" else 32], "bfloat16")
        SEMAPHORES.append("a%d_%d" % (_e, _c))


def layout(nodes):
    users = [[] for _ in nodes]
    for n in nodes:
        for d in n["deps"]:
            users[d["i"]].append(n)
    for n in reversed(nodes):
        n["cp"] = min(n["dur"].values()) + n["lat"] + max([WAKE + u["cp"] for u in users[n["i"]]] + [0.0])
    free = {"v": 0.0, "p": 0.0, "s": 0.0, "k": 0.0, "y": 0.0}
    left = list(nodes)
    order = []
    while left:
        best = None
        for q in sorted(free):
            cand = []
            for n in left:
                if q in n["dur"] and (n.get("prev") is None or "end" in n["prev"]) and all("end" in d for d in n["deps"]):
                    cand.append((max([d["end"] + WAKE for d in n["deps"]] + [0.0]), n))
            if not cand:
                continue
            t0 = max(free[q], min(c[0] for c in cand))
            t, n = min([(-c[1]["cp"] - c[1].get("pri", 0.0), c[1]["i"], max(t0, c[0]), c[1]) for c in cand if c[0] <= t0])[2:]
            key = (t, t + n["dur"][q], n["i"])
            if best is None or key < best[0]:
                best = (key, q, n)
        (t, e, _), q, n = best
        n["q"], n["start"], n["end"] = q, t, e + n["lat"]
        free[q] = e
        left.remove(n)
        order.append(n)
    return order


def rank_program(g, core, T, topo):
    r = T.rank_of(core)
    if r is None:
        return
    cores = T.cores
    queues = {"v": g.vector, "p": g.tensor, "s": g.scalar, "k": g, "y": g.sync}
    nodes = []

    def node(dur, deps, emit, sem=None, n=1, lat=0.0):
        flat = []
        for d in deps:
            if isinstance(d, list):
                flat += [x for x in d if x is not None]
            elif d is not None:
                flat.append(d)
        x = {"i": len(nodes), "dur": dur, "deps": flat, "emit": emit, "sem": sem, "n": n, "lat": lat}
        nodes.append(x)
        return x

    def V(deps, name, *a, cy=64):
        f = {"copy": g.vector.tensor_copy, "ts": g.vector.tensor_scalar, "tr": g.vector.transpose,
             "set": g.vector.memset}[name]
        return node({"v": FIX + max(cy, 64) * CYC}, deps, lambda q: f(*a))

    def VS(deps, out, in_, vcy, scy, on="vs"):
        def emit(q):
            if q == "v":
                return g.vector.tensor_copy(out, in_)
            return g.scalar.activation(out, in_, COPY)
        dur = {"v": FIX + vcy * CYC, "s": FIX + 0.015 + scy * CYC}
        return node({q: dur[q] for q in on}, deps, emit)

    def scaled(deps, out, in_, col):
        def emit(q):
            if q == "v":
                return g.vector.tensor_scalar(out, in_, col, None, OP.mult)
            return g.scalar.activation(out, in_, COPY, scale=col)
        return node({"v": FIX + 64 * CYC, "s": FIX + 0.015 + 128 * CYC}, deps, emit)

    def MM(deps, calls):
        def emit(q):
            for out, lhs, rhs, st, sp, cy in calls:
                x = g.tensor.matmul(out, lhs, rhs, st, sp)
            return x
        return node({"p": 0.02 + sum([c[5] for c in calls]) * PEC}, deps, emit)

    def TR(deps, calls):
        def emit(q):
            for out, in_ in calls:
                x = g.tensor.transpose(out, in_, T.ident[:])
            return x
        return node({"p": 0.02 + 128 * PEC * len(calls)}, deps, emit)

    def dma(q, deps, out, in_, s, more=0.0, pri=0.0):
        x = node({q: 0.05}, deps, lambda qq: queues[qq].dma_start(out, in_), s, 16, DMA + more)
        x["pri"] = pri
        return x

    def iota(out, n, pattern, base, cm):
        return node({"k": 0.13 + 2 * n * CYC}, [], lambda q: g.iota(out, pattern, base, cm, allow_small_or_imprecise_dtypes=True))

    d_gd = dma("s", [], T.gd[0], T.give[:], "gd")
    d_give = dma("s", [], T.gi[:], T.give[:], "gs")
    d_x = [dma("y", [], T.xi[:, 256 * h:256 * h + 256], T.x[:, 256 * h:256 * h + 256], "x%d" % h, 0.1 * h) for h in range(2)]
    d_wire = dma("s", [], T.wi[:], T.wires[:], "wl")
    tabs = [[], [], []]

    def load_table(l, h, n, more, deps=()):
        tabs[l].append(dma("y", list(deps), T.tab[16 * h:16 * h + 16 * n, l, :], T.tb[h:h + n, l * 65536:(l + 1) * 65536],
                           "t%d%d" % (l, h // n % 4), more, -1000.0))

    for h in (0, 2, 4):
        load_table(0, h, 2, 1.5 + 0.4 * h)

    s0 = 32 if r % 2 == 0 else -32
    s1 = 64 if r < 2 else -64
    k_pint = node({"k": 0.13}, [], lambda q: g.iota(T.pint[:, 0:1], [[0, 1]], 0, 1))
    k_pf = iota(T.pf[:], 1, [[0, 1]], 0, 1)
    k_jc = iota(T.jc[:], 128, [[1, 128]], 0, 0)
    k_jl = iota(T.jl[:], 128, [[-s1, 2], [-s0, 2], [1, 32]], 32 * (r ^ 3), 0)
    k_jr = iota(T.jr[:], 128, [[s1, 2], [s0, 2], [1, 32]], 32 * r, 0)
    c_pz = V([], "set", T.pall[:], 0.0, cy=256)
    c_ones = V([], "set", T.ones[:], 1.0)
    c_lo = V([k_pint], "ts", T.pint[:, 2:3], T.pint[:, 0:1], 15, None, OP.bitwise_and)
    c_low = V([c_lo], "copy", T.plow[:], T.pint[:, 2:3])
    c_id = V([k_jc, k_pf], "ts", T.ident[:], T.jc[:], T.pf[:], None, OP.is_equal)
    c_id4 = V([k_jc, k_pf], "ts", T.id4[:], T.jc[:], T.pf[:], None, OP.is_equal)
    c_m16 = V([k_jc, c_low], "ts", T.m16[:], T.jc[:, 0:16], T.plow[:], None, OP.is_equal)
    c_pall = []
    for x2 in range(2):
        for g2 in range(2):
            c_pall.append(V([c_id4, c_pz], "copy", T.pall[:, x2, g2, :, x2, :], T.id4[:, :, g2, :]))

    dst = {d: cores[r ^ d] for d in (1, 2, 3)}
    far = [d for d in dst if topo.chip(dst[d]) != topo.chip(core)]
    near = [d for d in dst if d not in far]
    use = {}
    farset = set()
    for j, d in enumerate(far):
        en = topo.engines(core, dst[d])
        farset |= set(en)
        w = len(en) // len(far)
        use[d] = en[j * w:j * w + w]
    for j, d in enumerate(near):
        en = [x for x in topo.engines(core, dst[d]) if x not in farset]
        w = len(en) // len(near)
        use[d] = en[j * w:j * w + w]
    total_eng = sum(len(use[d]) for d in dst)

    def send(deps, name, src, dest):
        def emit(q):
            tr = []
            for d in (1, 2, 3):
                rid, pid, _ = topo.addr(dst[d])
                tr.append(RemoteDMATransfer(dst_ids=[DstId(rid=rid, pnc=pid)], dma_engine_mask=sum(1 << x for x in use[d]),
                                            remote_sem=T.sem[name], src=src(d), dst=dest(d)))
            g.remote_dma_fused(tr, local_sem=T.sem.loc)
            return None
        return node({"k": 0.6}, deps, emit, name, total_eng, REM - 0.6)

    arr, own = {}, {}
    free = {"pr": None, "pl": None, "pw": None, "pv": None, "pa": None, "pm0": None, "pm1": None, "q1": None}
    a_give = send([d_gd], "ga", lambda d: T.gd[0], lambda d: T.gd[d])

    xb, xt = [], []
    for k in range(NBLK):
        xb.append(V([d_x[k // 2]], "copy", T.xb[:, 128 * k:128 * k + 128], T.xi[:, 128 * k:128 * k + 128], cy=128))
        xt.append(V([xb[k]], "tr", T.xt[:, k], T.xb[:, 128 * k:128 * k + 128]))

    c_gl = V([d_give], "copy", T.gl[:], T.gi[:])
    c_dg = V([c_gl, k_jr, k_pf], "ts", T.dg[:], T.jr[:], T.pf[:], T.gl[:, 0:1], OP.is_equal, OP.mult)
    a = MM([c_dg, c_ones], [(T.pw[:, 0:128], T.ones[:], T.dg[:], True, True, 128)])
    free["pw"] = c_one = V([a, k_pf], "ts", T.one[:], T.pw[:, 0:128], T.pf[:], None, OP.is_equal, cy=128)

    def zslot(e, k):
        for ci, blks in enumerate(SENDS[e]):
            if k in blks:
                return T["z%d_%d" % (e, ci)], "a%d_%d" % (e, ci), blks.index(k), blks

    def post(e, k, deps, src, on):
        z, name, i, blks = zslot(e, k)
        if MODE[e] == "A":
            own[(e, k)] = c = VS(deps, z[:, 3, i, :], src, 128, 128, on)
        else:
            c = VS(deps, T.cu[:, k, :], src, 128, 128, on)
            a = MM([c, c_one, free["pl"]], [(T.pl[:, 0:128], T.cu[:, k, :], T.one[:], True, True, 128)])
            free["pl"] = own[(e, k)] = VS([a], z[:, 3:7, i, :], T.pl[:, 0:128], 128, 128)
        if k == blks[-1]:
            n = send([own[(e, b)] for b in blks], name, lambda d: z[:, 3 if MODE[e] == "A" else 3 + d, :, :], lambda d: z[:, 3 - d, :, :])
            for b in blks:
                arr[(e, b)] = n
        return c

    for k in range(NBLK):
        a = MM([xt[k], c_pall, free["q1"]], [(T.q1[:, 0:4, bp, :], T.pall[:, g2, bp], T.xt[:, k, :, g2, :], g2 == 0, g2 == 1, 64)
                                             for bp in range(2) for g2 in range(2)])
        free["q1"] = post(0, k, [a], T.q1[:, 0:4], "s" if k == 0 else "vs")
    load_table(0, 6, 2, 2.5, [own[(0, 1)]])

    X = {}
    d_gg = [dma("y", [a_give if j < 3 else None], T.gg[32 * j:32 * j + 32, :],
                T.gd[3 - j, 32 * r:32 * r + 32, :] if j < 3 else T.give[32 * r:32 * r + 32, :], "gg", 0.0, -500.0) for j in (3, 0, 1, 2)]
    c_gb = X["gb"] = V([d_gg], "copy", T.gbs[:], T.gg[:])
    c_wf = V([d_wire], "copy", T.wf[:], T.wi[:])
    c_w = []
    for l in range(3):
        o0 = V([c_wf, k_jl], "ts", T.oh[:, 2 * l, :], T.jl[:], T.wf[:, 2 * l:2 * l + 1], 64.0, OP.is_equal, OP.mult)
        o1 = V([c_wf, k_jl], "ts", T.oh[:, 2 * l + 1, :], T.jl[:], T.wf[:, 2 * l + 1:2 * l + 2], None, OP.is_equal)
        b = ["pm1", "pm0", "pa"][l]
        a = MM([o0, o1, c_id, free[b]], [(T[b][:, 0:128], T.oh[:, 2 * l, :], T.ident[:], True, False, 128),
                                         (T[b][:, 0:128], T.oh[:, 2 * l + 1, :], T.ident[:], False, True, 128)])
        free[b] = c_wm = VS([a], T.wm[:, l, :], T[b][:, 0:128], 128, 128)
        if MODE[l] == "B":
            c_w.append([c_wm])
            continue
        c_og = X["og%d" % l] = V([c_gb, k_jc], "ts", T.og[:, l, :], T.jc[:], T.gbs[:, l:l + 1], None, OP.is_equal)
        b = ["pw", "pv"][l % 2]
        X["wm%d" % l] = []
        a = free[b]
        for j in range(4):
            a = MM([c_wm, c_og, a], [(T[b][:, 128 * j:128 * j + 128], T.og[32 * j:32 * j + 32, l, :], T.wm[32 * j:32 * j + 32, l, :], True, True, 128)])
            X["wm%d" % l].append(a)
        free[b] = X["wc%d" % l] = VS([a], T.wc[:, l, :, :], T[b][:, 0:512], 512, 512, "s")
        c_w.append([free[b]])
    c_msk = [scaled([c_m16, c_id], T.msk[:, u, :], T.ident[:], T.m16[:, u:u + 1]) for u in range(16)]

    B = []
    for t in range(NT):
        l, k = divmod(t, NBLK)
        pm = "pm%d" % (t % 2)
        o = {}
        B.append(o)
        for q in EXTRA.get(t, {}):
            o["x" + q] = []
            for n in EXTRA[t][q]:
                o["x" + q] += X[n] if isinstance(X[n], list) else [X[n]]
        z, _, i, blks = zslot(l, k)
        if MODE[l] == "A":
            o["a"] = MM([arr[(l, k)], own[(l, k)], c_w[l], free["pa"]],
                        [(T.pa[:, 0:128], T.wc[:, l, j, :], z[:, j, i, :], j == 3, j == 2, 128) for j in (3, 0, 1, 2)])
        else:
            o["tr"] = TR([arr[(l, k)], own[(l, k)], free["pr"], c_id],
                         [(T.pr[:, 0, :], z[:, 0:4, 0, :])] if len(blks) == 1 else [(T.pr[32 * j:32 * j + 32, 0, :], z[:, j, i, :]) for j in range(4)])
            o["lt"] = free["pr"] = VS([o["tr"]], T.lt[:, t, :], T.pr[:, 0, :], 64, 128, "v")
            o["a"] = MM([o["lt"], c_w[l], free["pa"]], [(T.pa[:, 0:128], T.wm[:, l, :], T.lt[:, t, :], True, True, 128)])
        o["off"] = free["pa"] = V([o["a"]], "copy", T.off[:, t, :], T.pa[:, 0:128], cy=128)
        if t == 0:
            for l2 in (1, 2):
                for h in range(8):
                    load_table(l2, h, 1, 0.6, [arr[(0, 0)] if l2 == 1 and h < TQ[1] else (tabs[1] + tabs[2])[-TQ[l2]]])

        def gather(q, b, n):
            x = VS([o["off"], tabs[l]], T.gt[:, t, 16 * b:16 * b + 16 * n], T.tab[:, l, :].indirect(T.off[:, t, b:b + n]),
                   16 * n * GAT / CYC, 16 * n * GAT / CYC, q)
            j = 1 if "g%s0" % q in o else 0
            o["g%s%d" % (q, j)] = x
            return x

        ms = []
        for h, (lo, w, calls) in enumerate(pieces(t)):
            gs = [gather(q, b, n) for q, b, n in calls]
            o["m%d" % h] = MM([gs, free[pm], c_msk],
                              [(T[pm][:, lo:lo + w], T.msk[:, u, :], T.gt[:, t, 16 * lo + u:16 * lo + 16 * w:16], u == 0, u == 15, max(64, w))
                               for u in range(16)])
            ms.append(o["m%d" % h])
        if l < 2:
            o["pms"] = free[pm] = post(l + 1, k, ms, T[pm][:, 0:128], "v")
        else:
            o["pms"] = free[pm] = VS(ms, T.pms[:, k], T[pm][:, 0:128], 128, 128, "v")
            o["otr"] = MM([o["pms"], free["q1"], c_pall], [(T.q1[:, 0:4, g2, :], T.pall[:, x2, g2], T.pms[:, k, :, x2, :], x2 == 0, x2 == 1, 64)
                                                           for g2 in range(2) for x2 in range(2)])
            o["z"] = free["q1"] = V([o["otr"]], "tr", T.yo[:, 128 * k:128 * k + 128], T.q1[:, 0:4], cy=128)
            dma("y", [o["z"]], T.y[:, 128 * k:128 * k + 128], T.yo[:, 128 * k:128 * k + 128], "yd")
    last = {}

    def then(q, *names):
        for t, name in names:
            if 0 <= t < NT and name in B[t]:
                x = B[t][name]
                for n in (x if isinstance(x, list) else [x]):
                    if q in n["dur"]:
                        n["prev"] = last.get(q)
                        last[q] = n

    way = [c_gl, xb[0], c_dg, xt[0], c_one, xb[1]]
    for n, p in zip(way[1:], way):
        n["prev"] = p
    for n in c_msk:
        n["prev"] = own[(0, 0)]
    then("v", (0, "lt"), (0, "off"))
    then("p", (0, "tr"), (0, "a"))
    for t in range(NT + 1):
        steps(then, t)

    order = layout(nodes)
    total = {}
    for n in order:
        s = n["sem"] or n["q"]
        total[s] = total.get(s, 0) + n["n"]
        n["tok"] = (s, total[s])
    waited = {}

    def wait(q, s, val):
        if waited.get((q, s), 0) < val:
            queues[q].wait_ge(T.sem[s], val)
            waited[(q, s)] = val

    sent = 0
    for n in order:
        need = {}
        for d in n["deps"]:
            s, val = d["tok"]
            need[s] = max(need.get(s, 0), val)
        for s in sorted(need):
            wait(n["q"], s, need[s])
        x = n["emit"](n["q"])
        if x is None:
            sent += n["n"]
        else:
            x.then_inc(T.sem[n["tok"][0]], n["n"])
    for s in sorted(total):
        wait("y", s, total[s])
    wait("y", "loc", sent)
